import numpy as np, ml_dtypes
CORES = [7,391,135,263,15,399,143,271]
N = 8
TK = 128
COEF = [[2,-1,0,0,1,0,0,-1],[-1,2,-1,0,0,1,0,0],[0,-1,2,-1,0,0,1,0],[0,0,-1,2,-1,0,0,1],[1,0,0,-1,2,-1,0,0],[0,1,0,0,-1,2,-1,0],[0,0,1,0,0,-1,2,-1],[-1,0,0,1,0,0,-1,2]]
def setup_inputs(rng):
    return {"x": rng.standard_normal((N, 128, TK), dtype=np.float32).astype(ml_dtypes.bfloat16), "a": (rng.standard_normal((N, 128, 128), dtype=np.float32) / 11).astype(ml_dtypes.bfloat16)}
def setup_inputs_big(rng):
    d = setup_inputs(rng)
    for k in ("x", "a"): d[k] = (d[k].astype(np.float32) * 1024.0).astype(d[k].dtype)
    return d
def setup_inputs_small(rng):
    d = setup_inputs(rng)
    for k in ("x", "a"): d[k] = (d[k].astype(np.float32) * (1 / 1024.0)).astype(d[k].dtype)
    return d
def setup_inputs_apart(rng):
    d = setup_inputs(rng)
    f = (10.0 ** rng.permutation(np.linspace(-1.5, 1.5, N))).astype(np.float32).reshape(N, 1, 1)
    for k in ("x", "a"): d[k] = (d[k].astype(np.float32) * f).astype(d[k].dtype)
    return d
def reference(x, a):
    X, A = x.astype(np.float64), a.astype(np.float64)
    y = np.stack([A[r].T @ sum(COEF[r][j] * X[j] for j in range(N)) for r in range(N)])
    return {"y": y.astype(ml_dtypes.bfloat16)}

from concourse.bass import DstId, RemoteDMATransfer
from concourse.mybir import AluOpType

P, W = 128, 128
BF = "bfloat16"

SCRATCH = {
    "xd":   ("dram", [P, W], BF),
    "hold": ("dram", [P, W], BF),
    "xs":   ("sbuf", [P, W], BF),
    "aa":   ("sbuf", [P, W], BF),
    "cst":  ("sbuf", [P, 2 * W], BF),
    "asc":  ("sbuf", [P, 2 * W], BF),
    "in0":  ("sbuf", [P, W], BF),
    "in1":  ("sbuf", [P, W], BF),
    "in2":  ("sbuf", [P, W], BF),
    "yb":   ("sbuf", [P, W], BF),
    "ps":   ("psum", [P, W], "float32"),
}
SEMAPHORES = ["ldx", "lds", "lda", "fill", "scal", "hop", "arr0", "arr1", "arr2", "sent", "mm", "cp", "st"]


def _links(topo, a, b):
    if topo.rack(topo.host(a)) == topo.rack(topo.host(b)):
        return 1 if (topo.mates(a, b) or topo.same_plane(a, b)) else 2
    return 1 if topo.chip(a) == topo.chip(b) else 3


def _plan(T, topo):
    cores, coef = T.cores, T.tables["COEF"]
    n = len(cores)
    direct, relayed = [], []
    for r in range(n):
        for j in range(n):
            if j == r or coef[r][j] == 0:
                continue
            if topo.may_write(cores[j], cores[r]):
                direct.append((j, r))
                continue
            cand = [q for q in range(n) if q != j and q != r
                    and topo.may_write(cores[j], cores[q]) and topo.may_write(cores[q], cores[r])]
            q = min(cand, key=lambda q: (_links(topo, cores[j], cores[q]) + _links(topo, cores[q], cores[r]),
                                         topo.rack(topo.host(cores[q])) != topo.rack(topo.host(cores[j])), q))
            relayed.append((j, q, r))
    return direct, relayed


def _engines(mask):
    return [e for e in range(mask.bit_length()) if (mask >> e) & 1]


def _bits(engines):
    return sum(1 << e for e in engines)


def rank_program(g, core, T, topo):
    me = T.rank_of(core)
    if me is None:
        return
    cores, coef, S = T.cores, T.tables["COEF"], T.sem
    direct, relayed = _plan(T, topo)

    def slot(j, r):
        return [a for a, b in direct if b == r].index(j)

    def hop_engines(j, q):
        return _engines(topo.mask(cores[j], cores[q]))[::2]

    def direct_engines(j, r):
        mine = [b for a, b in direct if a == j]
        return _engines(topo.mask(cores[j], cores[r]))[mine.index(r)::len(mine)]

    g.sync.dma_start(T.xd[:], T.x[:]).then_inc(S.ldx, 16)
    g.sync.dma_start(T.xs[:], T.x[:]).then_inc(S.lds, 16)
    g.sync.dma_start(T.aa[:], T.a[:]).then_inc(S.lda, 16)

    weights = sorted({c for c in coef[me] if c not in (0, 1)})
    blk = {c: slice(i * W, (i + 1) * W) for i, c in enumerate(weights)}
    for c in weights:
        g.vector.memset(T.cst[:, blk[c]], float(c)).then_inc(S.fill, 1)
    g.vector.wait_ge(S.fill, len(weights))
    g.vector.wait_ge(S.lda, 16)
    for c in weights:
        g.vector.tensor_tensor(T.asc[:, blk[c]], T.aa[:], T.cst[:, blk[c]], AluOpType.mult).then_inc(S.scal, 1)

    def lhs(c):
        return T.aa[:] if c == 1 else T.asc[:, blk[c]]

    sent = 0
    g.wait_ge(S.ldx, 16)
    for j, q, r in relayed:
        if j == me:
            rid, pid = topo.addr(cores[q], core)
            eng = hop_engines(j, q)
            g.remote_dma(T.hold[:], T.xd[:], S.hop, S.sent, pid, rid, _bits(eng))
            sent += len(eng)
    trs = []
    for j, r in direct:
        if j == me:
            rid, pid = topo.addr(cores[r], core)
            eng = direct_engines(j, r)
            k = slot(j, r)
            trs.append(RemoteDMATransfer(dst_ids=[DstId(rid=rid, pnc=pid)], dma_engine_mask=_bits(eng),
                                         remote_sem=S["arr%d" % k], src=T.xd[:], dst=T["in%d" % k][:]))
            sent += len(eng)
    g.remote_dma_fused(trs, local_sem=S.sent)
    for j, q, r in relayed:
        if q == me:
            g.wait_ge(S.hop, len(hop_engines(j, q)))
            rid, pid = topo.addr(cores[r], core)
            eng = _engines(topo.mask(core, cores[r]))
            g.remote_dma(T.in2[:], T.hold[:], S.arr2, S.sent, pid, rid, _bits(eng))
            sent += len(eng)
    g.wait_ge(S.sent, sent)

    terms = [(coef[me][j], T["in%d" % slot(j, me)], S["arr%d" % slot(j, me)], len(direct_engines(j, me)))
             for j, r in direct if r == me]
    terms += [(coef[me][j], T.in2, S.arr2, len(_engines(topo.mask(cores[q], core))))
              for j, q, r in relayed if r == me]
    g.tensor.wait_ge(S.lda, 16)
    g.tensor.wait_ge(S.scal, len(weights))
    g.tensor.wait_ge(S.lds, 16)
    g.tensor.matmul(T.ps[:], lhs(coef[me][me]), T.xs[:], True, False)
    for i, (c, buf, sem, cnt) in enumerate(terms):
        g.tensor.wait_ge(sem, cnt)
        last = i == len(terms) - 1
        mmi = g.tensor.matmul(T.ps[:], lhs(c), buf[:], False, last)
        if last:
            mmi.then_inc(S.mm, 1)

    g.vector.wait_ge(S.mm, 1)
    g.vector.tensor_copy(T.yb[:], T.ps[:]).then_inc(S.cp, 1)
    g.sync.wait_ge(S.cp, 1)
    g.sync.dma_start(T.y[:], T.yb[:]).then_inc(S.st, 16)
    g.sync.wait_ge(S.st, 16)
